import numpy as np
import ml_dtypes


def mxq(x, axis, fmt="e4m3"):
    dtype, down = {"e4m3": (ml_dtypes.float8_e4m3fn, 7), "e5m2": (ml_dtypes.float8_e5m2, 14)}[fmt]
    v = np.moveaxis(np.asarray(x, np.float32).astype(ml_dtypes.bfloat16).astype(np.float64), axis, -1)
    blocks = v.reshape(v.shape[:-1] + (-1, 32))
    amax = np.abs(blocks).max(-1, keepdims=True)
    byte = np.maximum(np.where(amax > 0, np.frexp(amax)[1] - 1 + 127, 0) - down, 1)
    scale = np.exp2(byte - 127.0)
    codes = (blocks / scale).astype(np.float32).astype(dtype).astype(np.float64)
    return np.moveaxis((codes * scale).reshape(v.shape), -1, axis)


WIDE = False


def mx_kscale(k):
    if not WIDE:
        return np.ones(k)
    levels = np.array([10, -10, 5, -5, 0])
    if k % 512:
        return np.exp2(np.random.permutation(np.resize(levels, k // 32))).repeat(32)
    a = np.empty((k // 512, 16))
    for p in range(k // 512):
        a[p, :8] = np.random.permutation(np.resize(levels, 8))
        for g in range(8):
            far = levels[np.abs(levels - a[p, g]) >= 10]
            a[p, g + 8] = far[np.random.randint(len(far))]
    return np.exp2(a.ravel()).repeat(32)


def f64(x):
    return np.asarray(x).astype(np.float64)


def striped(idx):
    return np.tile(np.asarray(idx).reshape(-1, 16).T, (8, 1)).astype(np.uint16)


def unstriped(offs):
    return offs[:16].T.reshape(-1).astype(np.int64)


E2M1 = np.array([0.0, 0.5, 1.0, 1.5, 2.0, 3.0, 4.0, 6.0, -0.0, -0.5, -1.0, -1.5, -2.0, -3.0, -4.0, -6.0])


def pack_weight(w, fmt):
    k, n = w.shape
    w = f64(np.asarray(w, np.float32).astype(ml_dtypes.bfloat16)).reshape(k // 32, 32, n)
    amax = np.abs(w).max(1)
    if fmt == "e4m3":
        byte = np.frexp(amax)[1] - 1 + 127 - 7
    else:
        mant, ex = np.frexp(amax / 6.0)
        byte = np.where(mant > 0.5, ex, ex - 1) + 127
    byte = np.clip(np.where(amax > 0, byte, 1), 1, 254)
    scaled = (w * np.exp2(127.0 - byte)[:, None, :]).reshape(k, n).astype(np.float32)
    by_word = np.ascontiguousarray(scaled.reshape(k // 512, 128, 4, n).transpose(0, 1, 3, 2))
    if fmt == "e4m3":
        words = by_word.astype(ml_dtypes.float8_e4m3fn).view(np.uint8)
    else:
        c = by_word.astype(ml_dtypes.float4_e2m1fn).view(np.uint8) & 0xF
        words = (c[..., 0::2] | (c[..., 1::2] << 4)).reshape(k // 512, 128, 2 * n)
    return np.ascontiguousarray(words), np.ascontiguousarray(byte.astype(np.uint8).reshape(k // 512, 16, n))


def unpack_weight(words, scales, fmt):
    g, _, n = scales.shape
    words = np.ascontiguousarray(words).reshape(g, 128, n, -1)
    if fmt == "e4m3":
        vals = words.view(ml_dtypes.float8_e4m3fn).astype(np.float64)
    else:
        nib = np.empty((g, 128, n, 4), np.uint8)
        nib[..., 0::2] = words & 0xF
        nib[..., 1::2] = words >> 4
        vals = E2M1[nib]
    vals = vals * np.repeat(np.exp2(scales.astype(np.float64) - 127.0), 8, axis=1)[..., None]
    return vals.transpose(0, 1, 3, 2).reshape(g * 512, n)


def sigmoid(v):
    return 1.0 / (1.0 + np.exp(-v))


D, E, T, I, Q = 512, 512, 2048, 512, 128


def setup_inputs():
    n = np.random.standard_normal
    idx = np.random.permutation(T)[:I]
    fd = mx_kscale(D)
    fi = mx_kscale(I)
    ti = np.ones(T)
    ti[idx] = fi
    keysp = pack_weight(n((D, T)) / fd[:, None], "e4m3")
    return {
        "query": (n((D, Q)) * 0.4 / np.sqrt(D) * fd[:, None]).astype(np.float32),
        "dquery": (n((D, Q)) * 0.6 / np.sqrt(D) * fd[:, None]).astype(np.float32),
        "query2": (n((D, Q)) * 0.5 / np.sqrt(D) * fd[:, None]).astype(np.float32),
        "dquery2": (n((D, Q)) * 0.5 / np.sqrt(D) * fd[:, None]).astype(np.float32),
        "keys_words": keysp[0],
        "keys_scales": keysp[1],
        "age": np.tile(np.random.uniform(0.0, 2.0, T), (128, 1)).astype(np.float32),
        "grace": (np.random.uniform(0.7, 1.5, (Q, 1))).astype(np.float32),
        "os": (np.random.uniform(4.0, 16.0, (1, I)) * fi).astype(np.float32),
        "vals": (n((E, T)) / ti).astype(np.float32),
        "offs": striped(idx),
    }


def reference(query, dquery, query2, dquery2, keys_words, keys_scales, age, grace, os, vals, offs):
    idx = unstriped(offs)
    keysu = unpack_weight(keys_words, keys_scales, "e4m3")
    queryq = mxq(f64(query), 0, "e4m3")
    keysidxg = keysu[:, idx]
    a = queryq.T @ keysidxg
    dqueryq = mxq(f64(dquery), 0, "e4m3")
    ta = dqueryq.T @ keysidxg
    query2q = mxq(f64(query2), 0, "e4m3")
    b = query2q.T @ keysidxg
    dquery2q = mxq(f64(dquery2), 0, "e4m3")
    tb = dquery2q.T @ keysidxg
    r = np.exp(a - np.max(a, axis=1, keepdims=True))
    gt = sigmoid((b + f64(grace) - f64(age)[:1][:, idx]) * 3.0)
    p = r * gt
    tr = ta * r
    tgt = tb * 3.0 * gt * (1.0 - gt)
    tp = tr * gt + tgt * r
    tw = (tp - np.sum(tp, axis=1, keepdims=True) * p / np.sum(p, axis=1, keepdims=True)) / np.sum(p, axis=1, keepdims=True)
    wo1 = tw * f64(os)
    wt1 = wo1.T
    vt1 = f64(vals)[:, idx].T
    wt1q = mxq(wt1, 0, "e4m3")
    vt1q = mxq(vt1, 0, "e4m3")
    o = wt1q.T @ vt1q
    return o

@@ -1,0 +1,210 @@
+from contextlib import ExitStack
+
+import concourse.mybir as mybir
+from concourse.masks import make_identity
+
+F32 = mybir.dt.float32
+BF16 = mybir.dt.bfloat16
+I32 = mybir.dt.int32
+U32 = mybir.dt.uint32
+U16 = mybir.dt.uint16
+U8 = mybir.dt.uint8
+FP8X4 = mybir.dt.float8_e4m3fn_x4
+ACT = mybir.ActivationFunctionType
+ALU = mybir.AluOpType
+AXIS_X = mybir.AxisListType.X
+
+P = 128
+PACK = 4
+D, E, T, I, Q = 512, 512, 2048, 512, 128
+CHUNKS = I // P
+E_BLOCKS = E // P
+
+FLOPS = 4 * 2 * D * Q * I + 2 * I * Q * E
+BYTES = 4 * (4 * D * Q + T + Q + I + E * T + Q * E) + D * T + 16 * T + 2 * P * (I // 16)
+
+
+def tile_attend_ttsoftlives_kernel(tc, query, dquery, query2, dquery2, keys_words, keys_scales, age, grace, slot_factor, vals, offs, out):
+    nc = tc.nc
+    with ExitStack() as ctx:
+        keep = ctx.enter_context(tc.tile_pool(name="keep", bufs=1))
+        psum = ctx.enter_context(tc.psum_pool(name="psum", bufs=1))
+
+        def sb(name, shape, dtype, tag=None):
+            return keep.tile(shape, dtype, name=name, tag=tag or name, align_bytes=64)
+
+        offsets = keep.tile([P, I // 16], U16, name="offsets")
+        nc.sync.dma_start(offsets[:], offs)
+
+        def load_query(name, src):
+            raw = sb(name + "_raw", [P, PACK, Q], F32)
+            nc.sync.dma_start(raw[:], src.rearrange("(p j) q -> p j q", j=PACK))
+            return raw
+
+        def load_vals(block):
+            window = sb("vals%d" % block, [P, T], F32)
+            nc.sync.dma_start(window[:], vals[block * P : (block + 1) * P, :])
+            return window
+
+        key_bytes = sb("key_bytes", [P, T], U8)
+        age_row = sb("age_row", [P, T], F32)
+        nc.vector.memset(age_row[0 : P - 1, :], 0.0)
+        nc.sync.dma_start(age_row[P - 1 : P, :], age[0:1, :])
+        os_cols = sb("os_cols", [P, PACK], F32)
+        nc.sync.dma_start(os_cols[:], slot_factor[0].rearrange("(p c) -> p c", c=PACK))
+        for quad in range(4):
+            rows = keys_scales[0, 4 * quad : 4 * quad + 4, :].bitcast(I32)
+            nc.sync.dma_start(key_bytes[32 * quad : 32 * quad + 32, :].bitcast(I32), rows.unsqueeze(0).broadcast_to([8, 4, T // 4]))
+        key_words = sb("key_words", [P, T], U32)
+        nc.sync.dma_start(key_words[:].bitcast(I32), keys_words[0].rearrange("p n t -> p (n t)").bitcast(I32))
+        q2_raw = load_query("q2", query2)
+        grace_col = sb("grace_col", [P, 1], F32)
+        nc.sync.dma_start(grace_col[:], grace)
+        q_raw = load_query("q", query)
+        dq2_raw = load_query("dq2", dquery2)
+        dq_raw = load_query("dq", dquery)
+        windows = [load_vals(block) for block in range(E_BLOCKS)]
+
+        ident = sb("ident", [P, P], F32)
+        make_identity(nc, ident[:])
+
+        warm_exp = sb("warm_exp", [P, 1], F32)
+        nc.scalar.activation(warm_exp[:], ident[:, 0:1], ACT.Sigmoid)
+
+        def quantize(name, grouped, width, reuse=None):
+            codes = sb(name + "_codes", [P, width], U32, tag=reuse)
+            scales = sb(name + "_scales", [P, width], U8)
+            nc.vector.quantize_mx(out=codes[:].bitcast(FP8X4), scales=scales[:], in_=grouped[:].rearrange("p w j -> p (w j)"))
+            return codes, scales
+
+        def mx(dst, lhs, rhs, lhs_cols=slice(None), rhs_cols=slice(None)):
+            nc.tensor.matmul_mx(
+                out=dst,
+                lhsT=lhs[0][:, lhs_cols].bitcast(FP8X4),
+                lhsT_scale=lhs[1][:, lhs_cols],
+                rhs=rhs[0][:, rhs_cols].bitcast(FP8X4),
+                rhs_scale=rhs[1][:, rhs_cols],
+                start=True,
+                stop=True,
+            )
+
+        def group_on_scalar(name, raw):
+            grouped = sb(name + "_grouped", [P, Q, PACK], BF16)
+            nc.scalar.copy(grouped[:], raw[:].rearrange("p j q -> p q j"))
+            return grouped
+
+        def group_on_vector(name, raw):
+            grouped = sb(name + "_grouped", [P, Q, PACK], BF16)
+            nc.vector.tensor_copy(grouped[:], raw[:].rearrange("p j q -> p q j"))
+            return grouped
+
+        def group_on_gpsimd(name, raw):
+            grouped = sb(name + "_grouped", [P, Q, PACK], BF16, tag="gate_slope")
+            nc.gpsimd.tensor_scalar(grouped[:], raw[:].rearrange("p j q -> p q j"), 1.0, 0.0, ALU.mult, ALU.add)
+            return grouped
+
+        def turn_pairs(grouped, rows, bank):
+            words = rows[:].bitcast(F32)
+            for u in range(2):
+                nc.tensor.transpose(bank[:, u, :], words[:, u : I // 2 : 2], ident[:])
+            nc.scalar.copy(grouped.rearrange("p w j -> p (w j)").bitcast(F32).rearrange("p (w u) -> p w u", u=2), bank[:].rearrange("p u w -> p w u"))
+
+        os_bank = psum.tile([P, PACK, P], F32, name="os_bank", tag="tb")
+        for c in range(PACK):
+            nc.tensor.transpose(os_bank[:, c, :], os_cols[:, c : c + 1].to_broadcast([P, P]), ident[:])
+        os_rows = sb("os_rows", [P, P, PACK], F32)
+        nc.scalar.copy(os_rows[:], os_bank[:].rearrange("p c n -> p n c"))
+
+        listed_age = sb("listed_age", [P, I], F32)
+        nc.vector.tensor_copy(listed_age[:], age_row[:].indirect(offsets[:]))
+        listed_bytes = sb("listed_bytes", [P, I], U8)
+        nc.vector.tensor_copy(listed_bytes[:], key_bytes[:].indirect(offsets[:]))
+        listed_words = sb("listed_words", [P, I], U32)
+        nc.vector.tensor_copy(listed_words[:], key_words[:].indirect(offsets[:]))
+        keys = (listed_words, listed_bytes)
+
+        age_bank = psum.tile([P, CHUNKS, P], F32, name="age_bank", tag="small")
+        for c in range(CHUNKS):
+            nc.tensor.transpose(age_bank[:, c, :], listed_age[:, c * P : (c + 1) * P], ident[:])
+        age_cols = sb("age_cols", [P, CHUNKS], F32)
+        nc.scalar.copy(age_cols[:], age_bank[:, :, P - 1])
+
+        age_spread = psum.tile([P, I], F32, name="age_spread", tag="ta")
+        for c in range(CHUNKS):
+            nc.tensor.transpose(age_spread[:, c * P : (c + 1) * P], age_cols[:, c : c + 1].to_broadcast([P, P]), ident[:])
+        age_rows = sb("age_rows", [P, I], F32)
+        nc.scalar.copy(age_rows[:], age_spread[:])
+
+        def scores(name, grouped):
+            bank = psum.tile([P, I], F32, name=name, tag=name)
+            mx(bank[:], quantize(name + "_rows", grouped, Q), keys)
+            return bank
+
+        b = scores("b", group_on_scalar("q2", q2_raw))
+        a = scores("a", group_on_scalar("q", q_raw))
+        dq2_grouped = group_on_vector("dq2", dq2_raw)
+        dq_grouped = group_on_gpsimd("dq", dq_raw)
+        life = sb("life", [P, I], F32)
+        nc.vector.scalar_tensor_tensor(life[:], b[:], grace_col[:], age_rows[:], ALU.add, ALU.subtract)
+        tb = scores("tb", dq2_grouped)
+        ta = scores("ta", dq_grouped)
+        gate = sb("gate", [P, I], F32)
+        nc.scalar.activation(gate[:], life[:], ACT.Sigmoid, scale=3.0)
+        neg_max = sb("neg_max", [P, 1], F32)
+        nc.vector.tensor_reduce(neg_max[:], a[:], AXIS_X, ALU.max, negate=True)
+        r = sb("r", [P, I], F32)
+        nc.scalar.activation(r[:], a[:], ACT.Exp, bias=neg_max[:])
+
+        gate_slope = sb("gate_slope", [P, I], F32)
+        nc.vector.scalar_tensor_tensor(gate_slope[:], gate[:], 1.0, tb[:], ALU.subtract, ALU.mult)
+        slope = sb("slope", [P, I], F32)
+        nc.vector.scalar_tensor_tensor(slope[:], gate_slope[:], -3.0, ta[:], ALU.mult, ALU.add)
+
+        def gather_vals(block, reuse, grouped):
+            listed = sb("listed_vals%d" % block, [P, I], BF16, tag=reuse)
+            nc.vector.tensor_copy(listed[:], windows[block][:].indirect(offsets[:]))
+            bank = psum.tile([P, 2, P], F32, name="v_bank%d" % block, tag="v%d" % (block % 2))
+            turn_pairs(grouped, listed, bank)
+
+        v01_grouped = sb("v01_grouped", [P, 2 * P, PACK], BF16)
+        gather_vals(0, "gate_slope", v01_grouped[:, :P, :])
+
+        p = sb("p", [P, I], F32)
+        p_sum = sb("p_sum", [P, 1], F32)
+        nc.vector.scalar_tensor_tensor(p[:], r[:], 1.0, gate[:], ALU.mult, ALU.mult, accum_out=p_sum[:])
+        inv = sb("inv", [P, 1], F32)
+        nc.vector.reciprocal(inv[:], p_sum[:])
+        slope_n = sb("slope_n", [P, I], F32)
+        nc.scalar.activation(slope_n[:], slope[:], ACT.Copy, scale=inv[:])
+        p_os = sb("p_os", [P, I], F32)
+        nc.gpsimd.tensor_tensor(p_os[:], p[:], os_rows[:].rearrange("p n c -> p (n c)"), ALU.mult)
+
+        gather_vals(1, "r", v01_grouped[:, P:, :])
+
+        weighted = sb("weighted", [P, I], F32)
+        mean_slope = sb("mean_slope", [P, 1], F32)
+        nc.vector.scalar_tensor_tensor(weighted[:], p[:], inv[:], slope_n[:], ALU.mult, ALU.mult, accum_out=mean_slope[:])
+        w = sb("w", [P, I], BF16)
+        nc.vector.scalar_tensor_tensor(w[:], slope_n[:], mean_slope[:], p_os[:], ALU.subtract, ALU.mult)
+        w_bank = psum.tile([P, 2, Q], F32, name="w_bank", tag="a")
+        w_grouped = sb("w_grouped", [P, Q, PACK], BF16)
+        turn_pairs(w_grouped[:], w, w_bank)
+
+        def emit(name, v_mx, first, width, tag, copy):
+            bank = psum.tile([Q, width], F32, name=name, tag=tag)
+            mx(bank[:], w_mx, v_mx)
+            staged = sb(name + "_staged", [Q, width], F32)
+            copy(staged[:], bank[:])
+            nc.sync.dma_start(out[:, first : first + width], staged[:])
+
+        v2_grouped = sb("v2_grouped", [P, P, PACK], BF16)
+        gather_vals(2, "slope_n", v2_grouped[:])
+        v01_mx = quantize("v01", v01_grouped, 2 * P, reuse="p_os")
+        w_mx = quantize("w", w_grouped, Q)
+        emit("out01", v01_mx, 0, 2 * P, "b", nc.scalar.copy)
+        v3_grouped = sb("v3_grouped", [P, P, PACK], BF16)
+        gather_vals(3, "w_grouped", v3_grouped[:])
+        v2_mx = quantize("v2", v2_grouped, P, reuse="vals3")
+        v3_mx = quantize("v3", v3_grouped, P)
+        emit("out2", v2_mx, 2 * P, P, "tb", nc.scalar.copy)
+        emit("out3", v3_mx, 3 * P, P, "small", nc.vector.tensor_copy)

@@ -93,13 +93,8 @@ def tile_attend_ttsoftlives_kernel(tc, query, dquery, query2, dquery2, keys_word
             nc.scalar.copy(grouped[:], raw[:].rearrange("p j q -> p q j"))
             return grouped
 
-        def group_on_vector(name, raw):
-            grouped = sb(name + "_grouped", [P, Q, PACK], BF16)
-            nc.vector.tensor_copy(grouped[:], raw[:].rearrange("p j q -> p q j"))
-            return grouped
-
         def group_on_gpsimd(name, raw):
-            grouped = sb(name + "_grouped", [P, Q, PACK], BF16, tag="gate_slope")
+            grouped = sb(name + "_grouped", [P, Q, PACK], BF16)
             nc.gpsimd.tensor_scalar(grouped[:], raw[:].rearrange("p j q -> p q j"), 1.0, 0.0, ALU.mult, ALU.add)
             return grouped
 
@@ -129,33 +124,33 @@ def tile_attend_ttsoftlives_kernel(tc, query, dquery, query2, dquery2, keys_word
         age_cols = sb("age_cols", [P, CHUNKS], F32)
         nc.scalar.copy(age_cols[:], age_bank[:, :, P - 1])
 
-        age_spread = psum.tile([P, I], F32, name="age_spread", tag="ta")
-        for c in range(CHUNKS):
-            nc.tensor.transpose(age_spread[:, c * P : (c + 1) * P], age_cols[:, c : c + 1].to_broadcast([P, P]), ident[:])
-        age_rows = sb("age_rows", [P, I], F32)
-        nc.scalar.copy(age_rows[:], age_spread[:])
-
         def scores(name, grouped):
             bank = psum.tile([P, I], F32, name=name, tag=name)
             mx(bank[:], quantize(name + "_rows", grouped, Q), keys)
             return bank
 
+        age_spread = psum.tile([P, I], F32, name="age_spread", tag="ta")
+        for c in range(CHUNKS):
+            nc.tensor.transpose(age_spread[:, c * P : (c + 1) * P], age_cols[:, c : c + 1].to_broadcast([P, P]), ident[:])
         b = scores("b", group_on_scalar("q2", q2_raw))
-        a = scores("a", group_on_scalar("q", q_raw))
-        dq2_grouped = group_on_vector("dq2", dq2_raw)
-        dq_grouped = group_on_gpsimd("dq", dq_raw)
-        life = sb("life", [P, I], F32)
-        nc.vector.scalar_tensor_tensor(life[:], b[:], grace_col[:], age_rows[:], ALU.add, ALU.subtract)
+        q_grouped = group_on_scalar("q", q_raw)
+        age_rows = sb("age_rows", [P, I], F32, tag="q_raw")
+        nc.scalar.copy(age_rows[:], age_spread[:])
+        dq2_grouped = group_on_gpsimd("dq2", dq2_raw)
+        a = scores("a", q_grouped)
         tb = scores("tb", dq2_grouped)
-        ta = scores("ta", dq_grouped)
+        dq_grouped = group_on_gpsimd("dq", dq_raw)
+        life = sb("life", [P, I], F32, tag="dq2_grouped")
+        nc.vector.scalar_tensor_tensor(life[:], b[:], grace_col[:], age_rows[:], ALU.add, ALU.subtract)
         gate = sb("gate", [P, I], F32)
         nc.scalar.activation(gate[:], life[:], ACT.Sigmoid, scale=3.0)
-        neg_max = sb("neg_max", [P, 1], F32)
+        neg_max = sb("neg_max", [P, 1], F32, tag="q_raw")
         nc.vector.tensor_reduce(neg_max[:], a[:], AXIS_X, ALU.max, negate=True)
-        r = sb("r", [P, I], F32)
+        r = sb("r", [P, I], F32, tag="dq2_grouped")
         nc.scalar.activation(r[:], a[:], ACT.Exp, bias=neg_max[:])
+        ta = scores("ta", dq_grouped)
 
-        gate_slope = sb("gate_slope", [P, I], F32)
+        gate_slope = sb("gate_slope", [P, I], F32, tag="dq_grouped")
         nc.vector.scalar_tensor_tensor(gate_slope[:], gate[:], 1.0, tb[:], ALU.subtract, ALU.mult)
         slope = sb("slope", [P, I], F32)
         nc.vector.scalar_tensor_tensor(slope[:], gate_slope[:], -3.0, ta[:], ALU.mult, ALU.add)
@@ -166,8 +161,8 @@ def tile_attend_ttsoftlives_kernel(tc, query, dquery, query2, dquery2, keys_word
             bank = psum.tile([P, 2, P], F32, name="v_bank%d" % block, tag="v%d" % (block % 2))
             turn_pairs(grouped, listed, bank)
 
-        v01_grouped = sb("v01_grouped", [P, 2 * P, PACK], BF16)
-        gather_vals(0, "gate_slope", v01_grouped[:, :P, :])
+        wv0_grouped = sb("wv0_grouped", [P, Q + P, PACK], BF16)
+        gather_vals(0, "dq_grouped", wv0_grouped[:, Q:, :])
 
         p = sb("p", [P, I], F32)
         p_sum = sb("p_sum", [P, 1], F32)
@@ -179,7 +174,8 @@ def tile_attend_ttsoftlives_kernel(tc, query, dquery, query2, dquery2, keys_word
         p_os = sb("p_os", [P, I], F32)
         nc.gpsimd.tensor_tensor(p_os[:], p[:], os_rows[:].rearrange("p n c -> p (n c)"), ALU.mult)
 
-        gather_vals(1, "r", v01_grouped[:, P:, :])
+        v12_grouped = sb("v12_grouped", [P, 2 * P, PACK], BF16)
+        gather_vals(1, "dq2_grouped", v12_grouped[:, :P, :])
 
         weighted = sb("weighted", [P, I], F32)
         mean_slope = sb("mean_slope", [P, 1], F32)
@@ -187,24 +183,25 @@ def tile_attend_ttsoftlives_kernel(tc, query, dquery, query2, dquery2, keys_word
         w = sb("w", [P, I], BF16)
         nc.vector.scalar_tensor_tensor(w[:], slope_n[:], mean_slope[:], p_os[:], ALU.subtract, ALU.mult)
         w_bank = psum.tile([P, 2, Q], F32, name="w_bank", tag="a")
-        w_grouped = sb("w_grouped", [P, Q, PACK], BF16)
-        turn_pairs(w_grouped[:], w, w_bank)
+        turn_pairs(wv0_grouped[:, :Q, :], w, w_bank)
 
-        def emit(name, v_mx, first, width, tag, copy):
-            bank = psum.tile([Q, width], F32, name=name, tag=tag)
-            mx(bank[:], w_mx, v_mx)
-            staged = sb(name + "_staged", [Q, width], F32)
-            copy(staged[:], bank[:])
-            nc.sync.dma_start(out[:, first : first + width], staged[:])
-
-        v2_grouped = sb("v2_grouped", [P, P, PACK], BF16)
-        gather_vals(2, "slope_n", v2_grouped[:])
-        v01_mx = quantize("v01", v01_grouped, 2 * P, reuse="p_os")
-        w_mx = quantize("w", w_grouped, Q)
-        emit("out01", v01_mx, 0, 2 * P, "b", nc.scalar.copy)
+        gather_vals(2, "slope_n", v12_grouped[:, P:, :])
         v3_grouped = sb("v3_grouped", [P, P, PACK], BF16)
-        gather_vals(3, "w_grouped", v3_grouped[:])
-        v2_mx = quantize("v2", v2_grouped, P, reuse="vals3")
+        gather_vals(3, "vals2", v3_grouped[:])
+        wv0_mx = quantize("wv0", wv0_grouped, Q + P, reuse="vals3")
+        v12_mx = quantize("v12", v12_grouped, 2 * P, reuse="wv0_grouped")
         v3_mx = quantize("v3", v3_grouped, P)
-        emit("out2", v2_mx, 2 * P, P, "tb", nc.scalar.copy)
-        emit("out3", v3_mx, 3 * P, P, "small", nc.vector.tensor_copy)
+
+        w_cols = slice(0, Q)
+        first = E - P
+        out_first = psum.tile([Q, first], F32, name="out_first", tag="b")
+        mx(out_first[:, :P], wv0_mx, wv0_mx, lhs_cols=w_cols, rhs_cols=slice(Q, Q + P))
+        mx(out_first[:, P:], wv0_mx, v12_mx, lhs_cols=w_cols)
+        staged_first = sb("staged_first", [Q, first], F32)
+        nc.scalar.copy(staged_first[:], out_first[:])
+        nc.sync.dma_start(out[:, :first], staged_first[:])
+        out_last = psum.tile([Q, P], F32, name="out_last", tag="small")
+        mx(out_last[:], wv0_mx, v3_mx, lhs_cols=w_cols)
+        staged_last = sb("staged_last", [Q, P], F32)
+        nc.vector.tensor_copy(staged_last[:], out_last[:])
+        nc.sync.dma_start(out[:, first:], staged_last[:])

@@ -47,16 +47,16 @@ def tile_attend_ttsoftlives_kernel(tc, query, dquery, query2, dquery2, keys_word
             return window
 
         key_bytes = sb("key_bytes", [P, T], U8)
+        nc.vector.memset(key_bytes[:].bitcast(I32), 0)
         age_row = sb("age_row", [P, T], F32)
-        nc.vector.memset(age_row[0 : P - 1, :], 0.0)
+        nc.vector.memset(age_row[0 : P - 1, : T // 2], 0.0)
         nc.sync.dma_start(age_row[P - 1 : P, :], age[0:1, :])
         os_cols = sb("os_cols", [P, PACK], F32)
         nc.sync.dma_start(os_cols[:], slot_factor[0].rearrange("(p c) -> p c", c=PACK))
-        for quad in range(4):
-            rows = keys_scales[0, 4 * quad : 4 * quad + 4, :].bitcast(I32)
-            nc.sync.dma_start(key_bytes[32 * quad : 32 * quad + 32, :].bitcast(I32), rows.unsqueeze(0).broadcast_to([8, 4, T // 4]))
         key_words = sb("key_words", [P, T], U32)
         nc.sync.dma_start(key_words[:].bitcast(I32), keys_words[0].rearrange("p n t -> p (n t)").bitcast(I32))
+        for row in range(4):
+            nc.sync.dma_start(key_bytes[row:P:32, :].bitcast(I32), keys_scales[0, row:16:4, :].bitcast(I32))
         q2_raw = load_query("q2", query2)
         grace_col = sb("grace_col", [P, 1], F32)
         nc.sync.dma_start(grace_col[:], grace)
@@ -67,6 +67,7 @@ def tile_attend_ttsoftlives_kernel(tc, query, dquery, query2, dquery2, keys_word
 
         ident = sb("ident", [P, P], F32)
         make_identity(nc, ident[:])
+        nc.gpsimd.memset(age_row[0 : P - 1, T // 2 :], 0.0)
 
         warm_exp = sb("warm_exp", [P, 1], F32)
         nc.scalar.activation(warm_exp[:], ident[:, 0:1], ACT.Sigmoid)
@@ -112,10 +113,10 @@ def tile_attend_ttsoftlives_kernel(tc, query, dquery, query2, dquery2, keys_word
 
         listed_age = sb("listed_age", [P, I], F32)
         nc.vector.tensor_copy(listed_age[:], age_row[:].indirect(offsets[:]))
-        listed_bytes = sb("listed_bytes", [P, I], U8)
-        nc.vector.tensor_copy(listed_bytes[:], key_bytes[:].indirect(offsets[:]))
         listed_words = sb("listed_words", [P, I], U32)
         nc.vector.tensor_copy(listed_words[:], key_words[:].indirect(offsets[:]))
+        listed_bytes = sb("listed_bytes", [P, I], U8)
+        nc.vector.tensor_copy(listed_bytes[:], key_bytes[:].indirect(offsets[:]))
         keys = (listed_words, listed_bytes)
 
         age_bank = psum.tile([P, CHUNKS, P], F32, name="age_bank", tag="small")

@@ -69,9 +69,6 @@ def tile_attend_ttsoftlives_kernel(tc, query, dquery, query2, dquery2, keys_word
         make_identity(nc, ident[:])
         nc.gpsimd.memset(age_row[0 : P - 1, T // 2 :], 0.0)
 
-        warm_exp = sb("warm_exp", [P, 1], F32)
-        nc.scalar.activation(warm_exp[:], ident[:, 0:1], ACT.Sigmoid)
-
         def quantize(name, grouped, width, reuse=None):
             codes = sb(name + "_codes", [P, width], U32, tag=reuse)
             scales = sb(name + "_scales", [P, width], U8)

from contextlib import ExitStack

import concourse.mybir as mybir
from concourse.masks import make_identity

F32 = mybir.dt.float32
BF16 = mybir.dt.bfloat16
I32 = mybir.dt.int32
U32 = mybir.dt.uint32
U16 = mybir.dt.uint16
U8 = mybir.dt.uint8
FP8X4 = mybir.dt.float8_e4m3fn_x4
ACT = mybir.ActivationFunctionType
ALU = mybir.AluOpType
AXIS_X = mybir.AxisListType.X

P = 128
PACK = 4
D, E, T, I, Q = 512, 512, 2048, 512, 128
CHUNKS = I // P
E_BLOCKS = E // P

FLOPS = 4 * 2 * D * Q * I + 2 * I * Q * E
BYTES = 4 * (4 * D * Q + T + Q + I + E * T + Q * E) + D * T + 16 * T + 2 * P * (I // 16)


def tile_attend_ttsoftlives_kernel(tc, query, dquery, query2, dquery2, keys_words, keys_scales, age, grace, slot_factor, vals, offs, out):
    nc = tc.nc
    with ExitStack() as ctx:
        keep = ctx.enter_context(tc.tile_pool(name="keep", bufs=1))
        psum = ctx.enter_context(tc.psum_pool(name="psum", bufs=1))

        def sb(name, shape, dtype, tag=None):
            return keep.tile(shape, dtype, name=name, tag=tag or name, align_bytes=64)

        offsets = keep.tile([P, I // 16], U16, name="offsets")
        nc.sync.dma_start(offsets[:], offs)

        def load_query(name, src):
            raw = sb(name + "_raw", [P, PACK, Q], F32)
            nc.sync.dma_start(raw[:], src.rearrange("(p j) q -> p j q", j=PACK))
            return raw

        def load_vals(block):
            window = sb("vals%d" % block, [P, T], F32)
            nc.sync.dma_start(window[:], vals[block * P : (block + 1) * P, :])
            return window

        key_bytes = sb("key_bytes", [P, T], U8)
        nc.vector.memset(key_bytes[:].bitcast(I32), 0)
        age_row = sb("age_row", [P, T], F32)
        nc.vector.memset(age_row[0 : P - 1, : T // 2], 0.0)
        nc.sync.dma_start(age_row[P - 1 : P, :], age[0:1, :])
        os_cols = sb("os_cols", [P, PACK], F32)
        nc.sync.dma_start(os_cols[:], slot_factor[0].rearrange("(p c) -> p c", c=PACK))
        key_words = sb("key_words", [P, T], U32)
        nc.sync.dma_start(key_words[:].bitcast(I32), keys_words[0].rearrange("p n t -> p (n t)").bitcast(I32))
        for row in range(4):
            nc.sync.dma_start(key_bytes[row:P:32, :].bitcast(I32), keys_scales[0, row:16:4, :].bitcast(I32))
        q2_raw = load_query("q2", query2)
        grace_col = sb("grace_col", [P, 1], F32)
        nc.sync.dma_start(grace_col[:], grace)
        q_raw = load_query("q", query)
        dq2_raw = load_query("dq2", dquery2)
        dq_raw = load_query("dq", dquery)
        windows = [load_vals(block) for block in range(E_BLOCKS)]

        ident = sb("ident", [P, P], F32)
        make_identity(nc, ident[:])
        nc.gpsimd.memset(age_row[0 : P - 1, T // 2 :], 0.0)

        def quantize(name, grouped, width, reuse=None):
            codes = sb(name + "_codes", [P, width], U32, tag=reuse)
            scales = sb(name + "_scales", [P, width], U8)
            nc.vector.quantize_mx(out=codes[:].bitcast(FP8X4), scales=scales[:], in_=grouped[:].rearrange("p w j -> p (w j)"))
            return codes, scales

        def mx(dst, lhs, rhs, lhs_cols=slice(None), rhs_cols=slice(None)):
            nc.tensor.matmul_mx(
                out=dst,
                lhsT=lhs[0][:, lhs_cols].bitcast(FP8X4),
                lhsT_scale=lhs[1][:, lhs_cols],
                rhs=rhs[0][:, rhs_cols].bitcast(FP8X4),
                rhs_scale=rhs[1][:, rhs_cols],
                start=True,
                stop=True,
            )

        def group_on_scalar(name, raw):
            grouped = sb(name + "_grouped", [P, Q, PACK], BF16)
            nc.scalar.copy(grouped[:], raw[:].rearrange("p j q -> p q j"))
            return grouped

        def group_on_gpsimd(name, raw):
            grouped = sb(name + "_grouped", [P, Q, PACK], BF16)
            nc.gpsimd.tensor_scalar(grouped[:], raw[:].rearrange("p j q -> p q j"), 1.0, 0.0, ALU.mult, ALU.add)
            return grouped

        def turn_pairs(grouped, rows, bank):
            words = rows[:].bitcast(F32)
            for u in range(2):
                nc.tensor.transpose(bank[:, u, :], words[:, u : I // 2 : 2], ident[:])
            nc.scalar.copy(grouped.rearrange("p w j -> p (w j)").bitcast(F32).rearrange("p (w u) -> p w u", u=2), bank[:].rearrange("p u w -> p w u"))

        os_bank = psum.tile([P, PACK, P], F32, name="os_bank", tag="tb")
        for c in range(PACK):
            nc.tensor.transpose(os_bank[:, c, :], os_cols[:, c : c + 1].to_broadcast([P, P]), ident[:])
        os_rows = sb("os_rows", [P, P, PACK], F32)
        nc.scalar.copy(os_rows[:], os_bank[:].rearrange("p c n -> p n c"))

        listed_age = sb("listed_age", [P, I], F32)
        nc.vector.tensor_copy(listed_age[:], age_row[:].indirect(offsets[:]))
        listed_words = sb("listed_words", [P, I], U32)
        nc.vector.tensor_copy(listed_words[:], key_words[:].indirect(offsets[:]))
        listed_bytes = sb("listed_bytes", [P, I], U8)
        nc.vector.tensor_copy(listed_bytes[:], key_bytes[:].indirect(offsets[:]))
        keys = (listed_words, listed_bytes)

        age_bank = psum.tile([P, CHUNKS, P], F32, name="age_bank", tag="small")
        for c in range(CHUNKS):
            nc.tensor.transpose(age_bank[:, c, :], listed_age[:, c * P : (c + 1) * P], ident[:])
        age_cols = sb("age_cols", [P, CHUNKS], F32)
        nc.scalar.copy(age_cols[:], age_bank[:, :, P - 1])

        def scores(name, grouped):
            bank = psum.tile([P, I], F32, name=name, tag=name)
            mx(bank[:], quantize(name + "_rows", grouped, Q), keys)
            return bank

        age_spread = psum.tile([P, I], F32, name="age_spread", tag="ta")
        for c in range(CHUNKS):
            nc.tensor.transpose(age_spread[:, c * P : (c + 1) * P], age_cols[:, c : c + 1].to_broadcast([P, P]), ident[:])
        b = scores("b", group_on_scalar("q2", q2_raw))
        q_grouped = group_on_scalar("q", q_raw)
        age_rows = sb("age_rows", [P, I], F32, tag="q_raw")
        nc.scalar.copy(age_rows[:], age_spread[:])
        dq2_grouped = group_on_gpsimd("dq2", dq2_raw)
        a = scores("a", q_grouped)
        tb = scores("tb", dq2_grouped)
        dq_grouped = group_on_gpsimd("dq", dq_raw)
        life = sb("life", [P, I], F32, tag="dq2_grouped")
        nc.vector.scalar_tensor_tensor(life[:], b[:], grace_col[:], age_rows[:], ALU.add, ALU.subtract)
        gate = sb("gate", [P, I], F32)
        nc.scalar.activation(gate[:], life[:], ACT.Sigmoid, scale=3.0)
        neg_max = sb("neg_max", [P, 1], F32, tag="q_raw")
        nc.vector.tensor_reduce(neg_max[:], a[:], AXIS_X, ALU.max, negate=True)
        r = sb("r", [P, I], F32, tag="dq2_grouped")
        nc.scalar.activation(r[:], a[:], ACT.Exp, bias=neg_max[:])
        ta = scores("ta", dq_grouped)

        gate_slope = sb("gate_slope", [P, I], F32, tag="dq_grouped")
        nc.vector.scalar_tensor_tensor(gate_slope[:], gate[:], 1.0, tb[:], ALU.subtract, ALU.mult)
        slope = sb("slope", [P, I], F32)
        nc.vector.scalar_tensor_tensor(slope[:], gate_slope[:], -3.0, ta[:], ALU.mult, ALU.add)

        def gather_vals(block, reuse, grouped):
            listed = sb("listed_vals%d" % block, [P, I], BF16, tag=reuse)
            nc.vector.tensor_copy(listed[:], windows[block][:].indirect(offsets[:]))
            bank = psum.tile([P, 2, P], F32, name="v_bank%d" % block, tag="v%d" % (block % 2))
            turn_pairs(grouped, listed, bank)

        wv0_grouped = sb("wv0_grouped", [P, Q + P, PACK], BF16)
        gather_vals(0, "dq_grouped", wv0_grouped[:, Q:, :])

        p = sb("p", [P, I], F32)
        p_sum = sb("p_sum", [P, 1], F32)
        nc.vector.scalar_tensor_tensor(p[:], r[:], 1.0, gate[:], ALU.mult, ALU.mult, accum_out=p_sum[:])
        inv = sb("inv", [P, 1], F32)
        nc.vector.reciprocal(inv[:], p_sum[:])
        slope_n = sb("slope_n", [P, I], F32)
        nc.scalar.activation(slope_n[:], slope[:], ACT.Copy, scale=inv[:])
        p_os = sb("p_os", [P, I], F32)
        nc.gpsimd.tensor_tensor(p_os[:], p[:], os_rows[:].rearrange("p n c -> p (n c)"), ALU.mult)

        v12_grouped = sb("v12_grouped", [P, 2 * P, PACK], BF16)
        gather_vals(1, "dq2_grouped", v12_grouped[:, :P, :])

        weighted = sb("weighted", [P, I], F32)
        mean_slope = sb("mean_slope", [P, 1], F32)
        nc.vector.scalar_tensor_tensor(weighted[:], p[:], inv[:], slope_n[:], ALU.mult, ALU.mult, accum_out=mean_slope[:])
        w = sb("w", [P, I], BF16)
        nc.vector.scalar_tensor_tensor(w[:], slope_n[:], mean_slope[:], p_os[:], ALU.subtract, ALU.mult)
        w_bank = psum.tile([P, 2, Q], F32, name="w_bank", tag="a")
        turn_pairs(wv0_grouped[:, :Q, :], w, w_bank)

        gather_vals(2, "slope_n", v12_grouped[:, P:, :])
        v3_grouped = sb("v3_grouped", [P, P, PACK], BF16)
        gather_vals(3, "vals2", v3_grouped[:])
        wv0_mx = quantize("wv0", wv0_grouped, Q + P, reuse="vals3")
        v12_mx = quantize("v12", v12_grouped, 2 * P, reuse="wv0_grouped")
        v3_mx = quantize("v3", v3_grouped, P)

        w_cols = slice(0, Q)
        first = E - P
        out_first = psum.tile([Q, first], F32, name="out_first", tag="b")
        mx(out_first[:, :P], wv0_mx, wv0_mx, lhs_cols=w_cols, rhs_cols=slice(Q, Q + P))
        mx(out_first[:, P:], wv0_mx, v12_mx, lhs_cols=w_cols)
        staged_first = sb("staged_first", [Q, first], F32)
        nc.scalar.copy(staged_first[:], out_first[:])
        nc.sync.dma_start(out[:, :first], staged_first[:])
        out_last = psum.tile([Q, P], F32, name="out_last", tag="small")
        mx(out_last[:], wv0_mx, v3_mx, lhs_cols=w_cols)
        staged_last = sb("staged_last", [Q, P], F32)
        nc.vector.tensor_copy(staged_last[:], out_last[:])
        nc.sync.dma_start(out[:, first:], staged_last[:])
